import numpy as np
import ml_dtypes


def mxq(x, axis, fmt="e4m3"):
    dtype, down = {"e4m3": (ml_dtypes.float8_e4m3fn, 7), "e5m2": (ml_dtypes.float8_e5m2, 14)}[fmt]
    v = np.moveaxis(np.asarray(x, np.float32).astype(ml_dtypes.bfloat16).astype(np.float64), axis, -1)
    blocks = v.reshape(v.shape[:-1] + (-1, 32))
    amax = np.abs(blocks).max(-1, keepdims=True)
    byte = np.maximum(np.where(amax > 0, np.frexp(amax)[1] - 1 + 127, 0) - down, 1)
    scale = np.exp2(byte - 127.0)
    codes = (blocks / scale).astype(np.float32).astype(dtype).astype(np.float64)
    return np.moveaxis((codes * scale).reshape(v.shape), -1, axis)


WIDE = False


def mx_kscale(k):
    if not WIDE:
        return np.ones(k)
    levels = np.array([10, -10, 5, -5, 0])
    if k % 512:
        return np.exp2(np.random.permutation(np.resize(levels, k // 32))).repeat(32)
    a = np.empty((k // 512, 16))
    for p in range(k // 512):
        a[p, :8] = np.random.permutation(np.resize(levels, 8))
        for g in range(8):
            far = levels[np.abs(levels - a[p, g]) >= 10]
            a[p, g + 8] = far[np.random.randint(len(far))]
    return np.exp2(a.ravel()).repeat(32)


def f64(x):
    return np.asarray(x).astype(np.float64)


def striped(idx):
    return np.tile(idx.reshape(-1, 16).T, (8, 1)).astype(np.uint16)


def unstriped(offs):
    return offs[:16].T.reshape(-1).astype(np.int64)


def pack_weight(w):
    k, n = w.shape
    w = f64(np.asarray(w, np.float32).astype(ml_dtypes.bfloat16)).reshape(k // 32, 32, n)
    amax = np.abs(w).max(1)
    byte = np.clip(np.where(amax > 0, np.frexp(amax)[1] - 1 + 127 - 7, 1), 1, 254)
    scaled = (w * np.exp2(127.0 - byte)[:, None, :]).reshape(k, n).astype(np.float32)
    words = np.ascontiguousarray(scaled.reshape(k // 512, 128, 4, n).transpose(0, 1, 3, 2)).astype(ml_dtypes.float8_e4m3fn).view(np.uint8)
    return words, np.ascontiguousarray(byte.astype(np.uint8).reshape(k // 512, 16, n))


def unpack_weight(words, scales):
    g, p, n, _ = words.shape
    vals = np.ascontiguousarray(words).view(ml_dtypes.float8_e4m3fn).astype(np.float64) * np.repeat(np.exp2(scales.astype(np.float64) - 127.0), 8, axis=1)[..., None]
    return vals.transpose(0, 1, 3, 2).reshape(g * 512, n)


E2M1 = np.array([0.0, 0.5, 1.0, 1.5, 2.0, 3.0, 4.0, 6.0, -0.0, -0.5, -1.0, -1.5, -2.0, -3.0, -4.0, -6.0])


def pack_fp4(w):
    k, n = w.shape
    w = f64(np.asarray(w, np.float32).astype(ml_dtypes.bfloat16)).reshape(k // 32, 32, n)
    amax = np.abs(w).max(1)
    mant, ex = np.frexp(amax / 6.0)
    byte = np.clip(np.where(amax > 0, np.where(mant > 0.5, ex, ex - 1) + 127, 1), 1, 254)
    scaled = (w * np.exp2(127.0 - byte)[:, None, :]).reshape(k, n).astype(np.float32)
    c = np.ascontiguousarray(scaled.reshape(k // 512, 128, 4, n).transpose(0, 1, 3, 2)).astype(ml_dtypes.float4_e2m1fn).view(np.uint8) & 0xF
    words = (c[..., 0::2] | (c[..., 1::2] << 4)).reshape(k // 512, 128, 2 * n)
    return np.ascontiguousarray(words), np.ascontiguousarray(byte.astype(np.uint8).reshape(k // 512, 16, n))


def unpack_fp4(words, scales):
    g, _, n = scales.shape
    words = np.ascontiguousarray(words).reshape(g, 128, n, 2)
    nib = np.empty((g, 128, n, 4), np.uint8)
    nib[..., 0::2] = words & 0xF
    nib[..., 1::2] = words >> 4
    vals = E2M1[nib] * np.repeat(np.exp2(scales.astype(np.float64) - 127.0), 8, axis=1)[..., None]
    return vals.transpose(0, 1, 3, 2).reshape(g * 512, n)


K, T, S, H, W, C, U = 512, 2048, 256, 512, 128, 512, 1024


def setup_inputs():
    n = np.random.standard_normal
    s = mx_kscale(K)[:, None]
    packed_xT = pack_weight(n((K, T)) * s)
    packed_w1 = pack_fp4(n((K, H)) / np.sqrt(K) / s)
    perm = np.random.permutation(S)
    return {
        "x_words": packed_xT[0],
        "x_scales": packed_xT[1],
        "w1_words": packed_w1[0],
        "w1_scales": packed_w1[1],
        "gs": (np.random.uniform(0.5, 1.5, (K, 1)) / s).astype(np.float32),
        "mem": n((C, U)).astype(np.float32),
        "offs": striped(np.random.permutation(T)[:S]),
        "n1": striped(perm[:W]),
        "n2": striped(perm[W:]),
        "n3": striped(np.random.permutation(S)),
        "cand": striped(np.random.permutation(T)[:C]),
        "n4": striped(np.random.permutation(U)[:S]),
    }


def reference(x_words, x_scales, w1_words, w1_scales, gs, mem, offs, n1, n2, n3, cand, n4):
    x_cand = unpack_weight(x_words, x_scales)[:, unstriped(cand)]
    xq = unpack_weight(x_words, x_scales)[:, unstriped(offs)]
    y = unpack_fp4(w1_words, w1_scales).T @ xq
    pa = y[:, unstriped(n1)]
    pb = y[:, unstriped(n2)]
    rb = np.minimum(pa, pb)
    ra = np.maximum(pa, pb)
    ds = np.zeros((H, S))
    ds[:, unstriped(n1)] = ra
    dt = ds.copy()
    dt[:, unstriped(n2)] = rb
    z = f64(gs) * (dt - dt[:, unstriped(n3)])
    s = 0.0625 * ((x_cand.T @ mxq(z, 0, "e4m3")))
    out = f64(mem).copy()
    out[:, unstriped(n4)] = s
    return out

@@ -1,0 +1,203 @@
+from contextlib import ExitStack
+
+import concourse.mybir as mybir
+
+F32 = mybir.dt.float32
+BF16 = mybir.dt.bfloat16
+I32 = mybir.dt.int32
+U32 = mybir.dt.uint32
+U16 = mybir.dt.uint16
+U8 = mybir.dt.uint8
+FP8X4 = mybir.dt.float8_e4m3fn_x4
+FP4X4 = mybir.dt.float4_e2m1fn_x4
+ALU = mybir.AluOpType
+COPY = mybir.ActivationFunctionType.Copy
+
+K, T, S, H, W, C, U = 512, 2048, 256, 512, 128, 512, 1024
+P = 128
+PACK = 4
+HALF = S // 2
+FLOPS = 2 * K * H * S + 2 * K * C * S
+
+
+def tile_picked_candorddpage_none_p_kernel(
+    tc, x_words, x_scales, w1_words, w1_scales, gs, mem, offs, n1, n2, n3, cand, n4, out
+):
+    nc = tc.nc
+    with ExitStack() as ctx:
+        lists = ctx.enter_context(tc.tile_pool(name="lists", bufs=1))
+        keep = ctx.enter_context(tc.tile_pool(name="keep", bufs=1))
+        psum = ctx.enter_context(tc.psum_pool(name="psum", bufs=1))
+
+        def load_list(src, name):
+            tile = lists.tile([P, src.shape[1]], U16, name=name)
+            nc.sync.dma_start(tile[:], src)
+            return tile
+
+        table_words = keep.tile([P, T], I32, align_bytes=64)
+        nc.sync.dma_start(table_words[:], x_words[0].rearrange("p n r -> p (n r)").bitcast(I32))
+        offs_t = load_list(offs, "offs_t")
+        w_scale_rows = keep.tile([P, H // 4], I32, tag="page3", align_bytes=64)
+        for q in range(4):
+            nc.scalar.dma_start(w_scale_rows[32 * q : 32 * q + 4, :], w1_scales[0, 4 * q : 4 * q + 4, :].bitcast(I32))
+        w_words_raw = keep.tile([P, 2 * H], U8, tag="page0", align_bytes=64)
+        nc.scalar.dma_start(w_words_raw[:].bitcast(I32), w1_words[0].bitcast(I32))
+        table_scales = keep.tile([P, T], U8, align_bytes=64)
+        nc.vector.memset(table_scales[:].bitcast(I32), 0)
+        for q in range(4):
+            nc.scalar.dma_start(
+                table_scales[32 * q : 32 * q + 4, :].bitcast(I32), x_scales[0, 4 * q : 4 * q + 4, :].bitcast(I32)
+            )
+        gain = keep.tile([P, PACK], F32)
+        nc.gpsimd.dma_start(gain[:], gs.rearrange("(p t) o -> p (t o)", t=PACK))
+        n1_t = load_list(n1, "n1_t")
+        n2_t = load_list(n2, "n2_t")
+        cand_t = load_list(cand, "cand_t")
+        n3_t = load_list(n3, "n3_t")
+        n4_t = load_list(n4, "n4_t")
+
+        neg_gain = keep.tile([P, PACK], F32)
+        nc.gpsimd.tensor_scalar(neg_gain[:], gain[:], -1.0, 0.0, ALU.mult, ALU.add)
+
+        w_scales_raw = keep.tile([P, H], U8, tag="page1", align_bytes=64)
+        nc.vector.memset(w_scales_raw[:].bitcast(I32), 0)
+        for q in range(4):
+            nc.vector.tensor_copy(w_scales_raw[32 * q : 32 * q + 4, :].bitcast(I32), w_scale_rows[32 * q : 32 * q + 4, :])
+        w_scales = keep.tile([P, PACK, P], U8, align_bytes=64)
+        nc.vector.tensor_copy(w_scales[:], w_scales_raw[:].rearrange("p (m t) -> p t m", t=PACK))
+        tok_scales = keep.tile([P, S], U8, align_bytes=64)
+        nc.vector.tensor_copy(tok_scales[:], table_scales[:].indirect(offs_t[:]))
+        w_words = []
+        for t in range(PACK):
+            dealt = keep.tile([P, P], U16, align_bytes=64, name=f"w_words{t}")
+            nc.scalar.copy(dealt[:], w_words_raw[:].bitcast(U16)[:, t::PACK])
+            w_words.append(dealt)
+
+        tok_words = keep.tile([P, S], U32, tag="page2", align_bytes=64)
+        nc.vector.tensor_copy(tok_words[:], table_words[:].bitcast(U32).indirect(offs_t[:]))
+
+        y = []
+        for t in range(PACK):
+            acc = psum.tile([P, S], F32, tag=f"bank{t}", name=f"y_acc{t}")
+            nc.tensor.matmul_mx(
+                out=acc[:],
+                lhsT=w_words[t][:].bitcast(FP4X4),
+                lhsT_scale=w_scales[:, t, :],
+                rhs=tok_words[:].bitcast(FP8X4),
+                rhs_scale=tok_scales[:],
+                start=True,
+                stop=True,
+            )
+            y_t = keep.tile([P, S], F32, name=f"y{t}")
+            nc.vector.tensor_copy(y_t[:], acc[:])
+            y.append(y_t)
+
+        pages = []
+        for c in range(C // P):
+            page = keep.tile([P, U], F32, tag=f"page{c}", align_bytes=64, name=f"page{c}")
+            nc.sync.dma_start(page[:], mem[c * P : (c + 1) * P, :])
+            pages.append(page)
+
+        pair, larger, smaller, dt, scaled = {}, {}, {}, {}, {}
+        z = {0: keep.tile([P, HALF, PACK], BF16, tag="z", align_bytes=64, name="z0")}
+
+        def fetch(t, which):
+            if which == 0:
+                pair[t] = keep.tile([P, 2, W], F32, tag=f"pair{t}", align_bytes=64, name=f"pair{t}")
+            nc.scalar.activation(pair[t][:, which, :], y[t][:].indirect((n1_t, n2_t)[which][:]), COPY)
+
+        def order(t):
+            larger[t] = keep.tile([P, W], F32, name=f"larger{t}")
+            smaller[t] = keep.tile([P, W], F32, tag=f"smaller{t}", name=f"smaller{t}")
+            nc.vector.tensor_tensor(larger[t][:], pair[t][:, 0, :], pair[t][:, 1, :], ALU.max)
+            nc.vector.tensor_tensor(smaller[t][:], pair[t][:, 0, :], pair[t][:, 1, :], ALU.min)
+
+        def put(t, which):
+            if which == 0:
+                dt[t] = keep.tile([P, S], F32, name=f"dt{t}")
+                nc.scalar.activation(dt[t][:].indirect(n1_t[:]), larger[t][:], COPY)
+            else:
+                nc.scalar.activation(dt[t][:].indirect(n2_t[:]), smaller[t][:], COPY)
+                scaled[t] = keep.tile([P, S], F32, name=f"scaled{t}")
+                nc.vector.tensor_scalar(scaled[t][:], dt[t][:], gain[:, t : t + 1], None, ALU.mult)
+
+        def diff(t, h, other):
+            nc.scalar.activation(other, dt[t][:].indirect(n3_t[:, 8 * h : 8 * h + 8]), COPY)
+            nc.vector.scalar_tensor_tensor(
+                z[h][:, :, t], other, neg_gain[:, t : t + 1], scaled[t][:, h * HALF : (h + 1) * HALF], ALU.mult, ALU.add
+            )
+
+        first = keep.tile([P, PACK, HALF], F32)
+        fetch(0, 0)
+        fetch(0, 1)
+        order(0)
+        fetch(1, 0)
+        fetch(1, 1)
+        order(1)
+        cand_words = keep.tile([P, C], U32, tag="pair0", align_bytes=64)
+        for i in range(2):
+            nc.vector.tensor_copy(
+                cand_words[:, 256 * i : 256 * (i + 1)], table_words[:].bitcast(U32).indirect(cand_t[:, 16 * i : 16 * (i + 1)])
+            )
+        put(0, 0)
+        fetch(2, 0)
+        put(0, 1)
+        fetch(2, 1)
+        order(2)
+        cand_scales = keep.tile([P, C], U8, tag="pair1", align_bytes=64)
+        nc.vector.tensor_copy(cand_scales[:], table_scales[:].indirect(cand_t[:]))
+        put(1, 0)
+        fetch(3, 0)
+        put(1, 1)
+        fetch(3, 1)
+        order(3)
+        diff(0, 0, first[:, 0, :])
+        put(2, 0)
+        diff(1, 0, first[:, 1, :])
+        put(2, 1)
+        put(3, 0)
+        diff(2, 0, first[:, 2, :])
+        put(3, 1)
+        diff(3, 0, first[:, 3, :])
+
+        scores = [keep.tile([P, S], F32, name=f"scores{c}") for c in range(C // P)]
+
+        def score(h):
+            codes = keep.tile([P, HALF], U32, align_bytes=64, name=f"z_codes{h}")
+            scales = keep.tile([P, HALF], U8, align_bytes=64, name=f"z_scales{h}")
+            nc.vector.quantize_mx(
+                out=codes[:].bitcast(FP8X4), scales=scales[:], in_=z[h][:].rearrange("p j t -> p (j t)")
+            )
+            for c in range(C // P):
+                acc = psum.tile([P, HALF], F32, tag=f"bank{(4 + 4 * h + c) % 8}", name=f"s_acc{h}_{c}")
+                nc.tensor.matmul_mx(
+                    out=acc[:],
+                    lhsT=cand_words[:, c * P : (c + 1) * P].bitcast(FP8X4),
+                    lhsT_scale=cand_scales[:, c * P : (c + 1) * P],
+                    rhs=codes[:].bitcast(FP8X4),
+                    rhs_scale=scales[:],
+                    start=True,
+                    stop=True,
+                )
+                if (h, c) == (0, 0):
+                    nc.scalar.activation(scores[c][:, :HALF], acc[:], COPY, scale=0.0625)
+                else:
+                    nc.vector.tensor_scalar(scores[c][:, h * HALF : (h + 1) * HALF], acc[:], 0.0625, None, ALU.mult)
+
+        score(0)
+        second = keep.tile([P, PACK, HALF], F32, tag="smaller3")
+        z[1] = keep.tile([P, HALF, PACK], BF16, tag="z", align_bytes=64, name="z1")
+        for t in range(PACK):
+            diff(t, 1, second[:, t, :])
+        score(1)
+
+        last = C // P - 1
+        for h in range(2):
+            for c in range(last):
+                nc.scalar.activation(
+                    pages[c][:].indirect(n4_t[:, 8 * h : 8 * h + 8]), scores[c][:, h * HALF : (h + 1) * HALF], COPY
+                )
+                if h == 1:
+                    nc.sync.dma_start(out[c * P : (c + 1) * P, :], pages[c][:])
+        nc.scalar.activation(pages[last][:].indirect(n4_t[:]), scores[last][:], COPY)
+        nc.sync.dma_start(out[last * P : (last + 1) * P, :], pages[last][:])

@@ -34,92 +34,107 @@ def tile_picked_candorddpage_none_p_kernel(
             nc.sync.dma_start(tile[:], src)
             return tile
 
+        scale_rows = keep.tile([P, T // 4], I32, align_bytes=64)
+
+        def load_rows(queue, tile, rows, q):
+            queue.dma_start(tile[32 * q : 32 * q + 4, :], rows[0, 4 * q : 4 * q + 4, :].bitcast(I32))
+
+        offs_t = load_list(offs, "offs_t")
+        for q in range(4):
+            load_rows((nc.scalar, nc.sync)[q // 2], scale_rows, x_scales, q)
         table_words = keep.tile([P, T], I32, align_bytes=64)
         nc.sync.dma_start(table_words[:], x_words[0].rearrange("p n r -> p (n r)").bitcast(I32))
-        offs_t = load_list(offs, "offs_t")
-        w_scale_rows = keep.tile([P, H // 4], I32, tag="page3", align_bytes=64)
+        w_scales_raw = keep.tile([P, H // 4], I32, align_bytes=64)
+        nc.vector.memset(w_scales_raw[:], 0)
+        table_scales = keep.tile([P, T // 4], I32, align_bytes=64)
+        nc.vector.memset(table_scales[:], 0)
         for q in range(4):
-            nc.scalar.dma_start(w_scale_rows[32 * q : 32 * q + 4, :], w1_scales[0, 4 * q : 4 * q + 4, :].bitcast(I32))
-        w_words_raw = keep.tile([P, 2 * H], U8, tag="page0", align_bytes=64)
+            load_rows(nc.scalar, w_scales_raw, w1_scales, q)
+        w_words_raw = keep.tile([P, 2 * H], U8, tag="w_stage", align_bytes=64)
         nc.scalar.dma_start(w_words_raw[:].bitcast(I32), w1_words[0].bitcast(I32))
-        table_scales = keep.tile([P, T], U8, align_bytes=64)
-        nc.vector.memset(table_scales[:].bitcast(I32), 0)
-        for q in range(4):
-            nc.scalar.dma_start(
-                table_scales[32 * q : 32 * q + 4, :].bitcast(I32), x_scales[0, 4 * q : 4 * q + 4, :].bitcast(I32)
-            )
+        n1_t = load_list(n1, "n1_t")
         gain = keep.tile([P, PACK], F32)
         nc.gpsimd.dma_start(gain[:], gs.rearrange("(p t) o -> p (t o)", t=PACK))
-        n1_t = load_list(n1, "n1_t")
         n2_t = load_list(n2, "n2_t")
         cand_t = load_list(cand, "cand_t")
         n3_t = load_list(n3, "n3_t")
         n4_t = load_list(n4, "n4_t")
+        pages = []
+        for c in range(C // P):
+            page = keep.tile([P, U], F32, name=f"page{c}")
+            nc.sync.dma_start(page[:], mem[c * P : (c + 1) * P, :])
+            pages.append(page)
 
         neg_gain = keep.tile([P, PACK], F32)
         nc.gpsimd.tensor_scalar(neg_gain[:], gain[:], -1.0, 0.0, ALU.mult, ALU.add)
 
-        w_scales_raw = keep.tile([P, H], U8, tag="page1", align_bytes=64)
-        nc.vector.memset(w_scales_raw[:].bitcast(I32), 0)
         for q in range(4):
-            nc.vector.tensor_copy(w_scales_raw[32 * q : 32 * q + 4, :].bitcast(I32), w_scale_rows[32 * q : 32 * q + 4, :])
-        w_scales = keep.tile([P, PACK, P], U8, align_bytes=64)
-        nc.vector.tensor_copy(w_scales[:], w_scales_raw[:].rearrange("p (m t) -> p t m", t=PACK))
+            nc.vector.tensor_copy(table_scales[32 * q : 32 * q + 4, :], scale_rows[32 * q : 32 * q + 4, :])
         tok_scales = keep.tile([P, S], U8, align_bytes=64)
-        nc.vector.tensor_copy(tok_scales[:], table_scales[:].indirect(offs_t[:]))
+        nc.vector.tensor_copy(tok_scales[:], table_scales[:].bitcast(U8).indirect(offs_t[:]))
+        tok_words = keep.tile([P, S], U32, align_bytes=64)
+        for h in range(2):
+            nc.vector.tensor_copy(
+                tok_words[:, h * HALF : (h + 1) * HALF], table_words[:].bitcast(U32).indirect(offs_t[:, 8 * h : 8 * h + 8])
+            )
         w_words = []
         for t in range(PACK):
-            dealt = keep.tile([P, P], U16, align_bytes=64, name=f"w_words{t}")
-            nc.scalar.copy(dealt[:], w_words_raw[:].bitcast(U16)[:, t::PACK])
-            w_words.append(dealt)
-
-        tok_words = keep.tile([P, S], U32, tag="page2", align_bytes=64)
-        nc.vector.tensor_copy(tok_words[:], table_words[:].bitcast(U32).indirect(offs_t[:]))
-
-        y = []
+            dealt_words = keep.tile([P, P], U16, align_bytes=64, name=f"w_words{t}")
+            nc.scalar.copy(dealt_words[:], w_words_raw[:].bitcast(U16)[:, t::PACK])
+            w_words.append(dealt_words)
+        first_scales = keep.tile([P, P], U8, align_bytes=64)
+        later_scales = keep.tile([P, PACK - 1, P], U8, tag="w_stage", align_bytes=64)
+        w_scales = [first_scales[:]] + [later_scales[:, t, :] for t in range(PACK - 1)]
         for t in range(PACK):
-            acc = psum.tile([P, S], F32, tag=f"bank{t}", name=f"y_acc{t}")
+            nc.vector.tensor_copy(w_scales[t], w_scales_raw[:].bitcast(U8)[:, t::PACK])
+
+        def project(t, cols, bank, y_t):
+            acc = psum.tile([P, cols.stop - cols.start], F32, tag=f"bank{bank}", name=f"y_acc{bank}")
             nc.tensor.matmul_mx(
                 out=acc[:],
                 lhsT=w_words[t][:].bitcast(FP4X4),
-                lhsT_scale=w_scales[:, t, :],
-                rhs=tok_words[:].bitcast(FP8X4),
-                rhs_scale=tok_scales[:],
+                lhsT_scale=w_scales[t],
+                rhs=tok_words[:, cols].bitcast(FP8X4),
+                rhs_scale=tok_scales[:, cols],
                 start=True,
                 stop=True,
             )
-            y_t = keep.tile([P, S], F32, name=f"y{t}")
-            nc.vector.tensor_copy(y_t[:], acc[:])
-            y.append(y_t)
-
-        pages = []
-        for c in range(C // P):
-            page = keep.tile([P, U], F32, tag=f"page{c}", align_bytes=64, name=f"page{c}")
-            nc.sync.dma_start(page[:], mem[c * P : (c + 1) * P, :])
-            pages.append(page)
-
-        pair, larger, smaller, dt, scaled = {}, {}, {}, {}, {}
-        z = {0: keep.tile([P, HALF, PACK], BF16, tag="z", align_bytes=64, name="z0")}
-
-        def fetch(t, which):
-            if which == 0:
-                pair[t] = keep.tile([P, 2, W], F32, tag=f"pair{t}", align_bytes=64, name=f"pair{t}")
-            nc.scalar.activation(pair[t][:, which, :], y[t][:].indirect((n1_t, n2_t)[which][:]), COPY)
-
-        def order(t):
-            larger[t] = keep.tile([P, W], F32, name=f"larger{t}")
-            smaller[t] = keep.tile([P, W], F32, tag=f"smaller{t}", name=f"smaller{t}")
-            nc.vector.tensor_tensor(larger[t][:], pair[t][:, 0, :], pair[t][:, 1, :], ALU.max)
-            nc.vector.tensor_tensor(smaller[t][:], pair[t][:, 0, :], pair[t][:, 1, :], ALU.min)
-
-        def put(t, which):
-            if which == 0:
-                dt[t] = keep.tile([P, S], F32, name=f"dt{t}")
-                nc.scalar.activation(dt[t][:].indirect(n1_t[:]), larger[t][:], COPY)
+            if t == 0:
+                nc.scalar.copy(y_t[:, cols], acc[:])
             else:
-                nc.scalar.activation(dt[t][:].indirect(n2_t[:]), smaller[t][:], COPY)
-                scaled[t] = keep.tile([P, S], F32, name=f"scaled{t}")
-                nc.vector.tensor_scalar(scaled[t][:], dt[t][:], gain[:, t : t + 1], None, ALU.mult)
+                nc.vector.tensor_copy(y_t[:, cols], acc[:])
+
+        y = [keep.tile([P, S], F32, name=f"y{t}") for t in range(PACK)]
+        project(0, slice(0, HALF), 7, y[0])
+        project(0, slice(HALF, S), 0, y[0])
+        for t in range(1, PACK):
+            project(t, slice(0, S), t, y[t])
+
+        pairs = []
+        for t in range(PACK):
+            pair = keep.tile([P, 2, W], F32, tag=f"pair{t}", align_bytes=64, name=f"pair{t}")
+            nc.scalar.activation(pair[:, 0, :], y[t][:].indirect(n1_t[:]), COPY)
+            nc.scalar.activation(pair[:, 1, :], y[t][:].indirect(n2_t[:]), COPY)
+            pairs.append(pair)
+
+        larger = [keep.tile([P, W], F32, name=f"larger{t}") for t in range(PACK)]
+        smaller = [keep.tile([P, W], F32, tag=f"smaller{t}", name=f"smaller{t}") for t in range(PACK)]
+        for couple in ((0, 1), (2, 3)):
+            for result, op in ((larger, ALU.max), (smaller, ALU.min)):
+                for t in couple:
+                    nc.vector.tensor_tensor(result[t][:], pairs[t][:, 0, :], pairs[t][:, 1, :], op)
+
+        cand_words = keep.tile([P, C], U32, tag="pair0", align_bytes=64)
+        for i in range(2):
+            nc.vector.tensor_copy(
+                cand_words[:, 256 * i : 256 * (i + 1)], table_words[:].bitcast(U32).indirect(cand_t[:, 16 * i : 16 * (i + 1)])
+            )
+        cand_scales = keep.tile([P, C], U8, tag="pair1", align_bytes=64)
+        nc.vector.tensor_copy(cand_scales[:], table_scales[:].bitcast(U8).indirect(cand_t[:]))
+
+        dt = [keep.tile([P, S], F32, name=f"dt{t}") for t in range(PACK)]
+        scaled = [keep.tile([P, S], F32, name=f"scaled{t}") for t in range(PACK)]
+        z = {0: keep.tile([P, HALF, PACK], BF16, tag="z", align_bytes=64, name="z0")}
 
         def diff(t, h, other):
             nc.scalar.activation(other, dt[t][:].indirect(n3_t[:, 8 * h : 8 * h + 8]), COPY)
@@ -128,37 +143,14 @@ def tile_picked_candorddpage_none_p_kernel(
             )
 
         first = keep.tile([P, PACK, HALF], F32)
-        fetch(0, 0)
-        fetch(0, 1)
-        order(0)
-        fetch(1, 0)
-        fetch(1, 1)
-        order(1)
-        cand_words = keep.tile([P, C], U32, tag="pair0", align_bytes=64)
-        for i in range(2):
-            nc.vector.tensor_copy(
-                cand_words[:, 256 * i : 256 * (i + 1)], table_words[:].bitcast(U32).indirect(cand_t[:, 16 * i : 16 * (i + 1)])
-            )
-        put(0, 0)
-        fetch(2, 0)
-        put(0, 1)
-        fetch(2, 1)
-        order(2)
-        cand_scales = keep.tile([P, C], U8, tag="pair1", align_bytes=64)
-        nc.vector.tensor_copy(cand_scales[:], table_scales[:].indirect(cand_t[:]))
-        put(1, 0)
-        fetch(3, 0)
-        put(1, 1)
-        fetch(3, 1)
-        order(3)
-        diff(0, 0, first[:, 0, :])
-        put(2, 0)
-        diff(1, 0, first[:, 1, :])
-        put(2, 1)
-        put(3, 0)
-        diff(2, 0, first[:, 2, :])
-        put(3, 1)
-        diff(3, 0, first[:, 3, :])
+        for couple in ((0, 1), (2, 3)):
+            for t in couple:
+                nc.scalar.activation(dt[t][:].indirect(n1_t[:]), larger[t][:], COPY)
+            for t in couple:
+                nc.scalar.activation(dt[t][:].indirect(n2_t[:]), smaller[t][:], COPY)
+                nc.vector.tensor_scalar(scaled[t][:], dt[t][:], gain[:, t : t + 1], None, ALU.mult)
+            for t in couple:
+                diff(t, 0, first[:, t, :])
 
         scores = [keep.tile([P, S], F32, name=f"scores{c}") for c in range(C // P)]
 

@@ -52,9 +52,9 @@ def tile_picked_candorddpage_none_p_kernel(
             load_rows(nc.scalar, w_scales_raw, w1_scales, q)
         w_words_raw = keep.tile([P, 2 * H], U8, tag="w_stage", align_bytes=64)
         nc.scalar.dma_start(w_words_raw[:].bitcast(I32), w1_words[0].bitcast(I32))
-        n1_t = load_list(n1, "n1_t")
         gain = keep.tile([P, PACK], F32)
-        nc.gpsimd.dma_start(gain[:], gs.rearrange("(p t) o -> p (t o)", t=PACK))
+        nc.scalar.dma_start(gain[:], gs.rearrange("(p t) o -> p (t o)", t=PACK))
+        n1_t = load_list(n1, "n1_t")
         n2_t = load_list(n2, "n2_t")
         cand_t = load_list(cand, "cand_t")
         n3_t = load_list(n3, "n3_t")
@@ -64,9 +64,6 @@ def tile_picked_candorddpage_none_p_kernel(
             page = keep.tile([P, U], F32, name=f"page{c}")
             nc.sync.dma_start(page[:], mem[c * P : (c + 1) * P, :])
             pages.append(page)
-
-        neg_gain = keep.tile([P, PACK], F32)
-        nc.gpsimd.tensor_scalar(neg_gain[:], gain[:], -1.0, 0.0, ALU.mult, ALU.add)
 
         for q in range(4):
             nc.vector.tensor_copy(table_scales[32 * q : 32 * q + 4, :], scale_rows[32 * q : 32 * q + 4, :])
@@ -132,14 +129,16 @@ def tile_picked_candorddpage_none_p_kernel(
         cand_scales = keep.tile([P, C], U8, tag="pair1", align_bytes=64)
         nc.vector.tensor_copy(cand_scales[:], table_scales[:].bitcast(U8).indirect(cand_t[:]))
 
+        neg_gain = keep.tile([P, PACK], F32, tag="pair2", align_bytes=64)
+        nc.vector.tensor_scalar(neg_gain[:], gain[:], -1.0, None, ALU.mult)
         dt = [keep.tile([P, S], F32, name=f"dt{t}") for t in range(PACK)]
         scaled = [keep.tile([P, S], F32, name=f"scaled{t}") for t in range(PACK)]
         z = {0: keep.tile([P, HALF, PACK], BF16, tag="z", align_bytes=64, name="z0")}
 
-        def diff(t, h, other):
+        def diff(t, h, other, result):
             nc.scalar.activation(other, dt[t][:].indirect(n3_t[:, 8 * h : 8 * h + 8]), COPY)
             nc.vector.scalar_tensor_tensor(
-                z[h][:, :, t], other, neg_gain[:, t : t + 1], scaled[t][:, h * HALF : (h + 1) * HALF], ALU.mult, ALU.add
+                result, other, neg_gain[:, t : t + 1], scaled[t][:, h * HALF : (h + 1) * HALF], ALU.mult, ALU.add
             )
 
         first = keep.tile([P, PACK, HALF], F32)
@@ -150,7 +149,7 @@ def tile_picked_candorddpage_none_p_kernel(
                 nc.scalar.activation(dt[t][:].indirect(n2_t[:]), smaller[t][:], COPY)
                 nc.vector.tensor_scalar(scaled[t][:], dt[t][:], gain[:, t : t + 1], None, ALU.mult)
             for t in couple:
-                diff(t, 0, first[:, t, :])
+                diff(t, 0, first[:, t, :], z[0][:, :, t])
 
         scores = [keep.tile([P, S], F32, name=f"scores{c}") for c in range(C // P)]
 
@@ -178,9 +177,13 @@ def tile_picked_candorddpage_none_p_kernel(
 
         score(0)
         second = keep.tile([P, PACK, HALF], F32, tag="smaller3")
-        z[1] = keep.tile([P, HALF, PACK], BF16, tag="z", align_bytes=64, name="z1")
+        planes = keep.tile([P, PACK, HALF], BF16, tag="z", align_bytes=64)
+        z[1] = keep.tile([P, HALF, PACK], BF16, align_bytes=64, name="z1")
         for t in range(PACK):
-            diff(t, 1, second[:, t, :])
+            diff(t, 1, second[:, t, :], planes[:, t, :])
+        nc.vector.tensor_copy(
+            z[1][:].rearrange("p (c i) t -> p c t i", i=4), planes[:].rearrange("p t (c i) -> p c t i", i=4)
+        )
         score(1)
 
         last = C // P - 1

@@ -195,4 +195,5 @@ def tile_picked_candorddpage_none_p_kernel(
                 if h == 1:
                     nc.sync.dma_start(out[c * P : (c + 1) * P, :], pages[c][:])
         nc.scalar.activation(pages[last][:].indirect(n4_t[:]), scores[last][:], COPY)
-        nc.sync.dma_start(out[last * P : (last + 1) * P, :], pages[last][:])
+        for queue, cols in ((nc.scalar, slice(0, U // 2)), (nc.sync, slice(U // 2, U))):
+            queue.dma_start(out[last * P : (last + 1) * P, cols], pages[last][:, cols])

from contextlib import ExitStack

import concourse.mybir as mybir

F32 = mybir.dt.float32
BF16 = mybir.dt.bfloat16
I32 = mybir.dt.int32
U32 = mybir.dt.uint32
U16 = mybir.dt.uint16
U8 = mybir.dt.uint8
FP8X4 = mybir.dt.float8_e4m3fn_x4
FP4X4 = mybir.dt.float4_e2m1fn_x4
ALU = mybir.AluOpType
COPY = mybir.ActivationFunctionType.Copy

K, T, S, H, W, C, U = 512, 2048, 256, 512, 128, 512, 1024
P = 128
PACK = 4
HALF = S // 2
FLOPS = 2 * K * H * S + 2 * K * C * S


def tile_picked_candorddpage_none_p_kernel(
    tc, x_words, x_scales, w1_words, w1_scales, gs, mem, offs, n1, n2, n3, cand, n4, out
):
    nc = tc.nc
    with ExitStack() as ctx:
        lists = ctx.enter_context(tc.tile_pool(name="lists", bufs=1))
        keep = ctx.enter_context(tc.tile_pool(name="keep", bufs=1))
        psum = ctx.enter_context(tc.psum_pool(name="psum", bufs=1))

        def load_list(src, name):
            tile = lists.tile([P, src.shape[1]], U16, name=name)
            nc.sync.dma_start(tile[:], src)
            return tile

        scale_rows = keep.tile([P, T // 4], I32, align_bytes=64)

        def load_rows(queue, tile, rows, q):
            queue.dma_start(tile[32 * q : 32 * q + 4, :], rows[0, 4 * q : 4 * q + 4, :].bitcast(I32))

        offs_t = load_list(offs, "offs_t")
        for q in range(4):
            load_rows((nc.scalar, nc.sync)[q // 2], scale_rows, x_scales, q)
        table_words = keep.tile([P, T], I32, align_bytes=64)
        nc.sync.dma_start(table_words[:], x_words[0].rearrange("p n r -> p (n r)").bitcast(I32))
        w_scales_raw = keep.tile([P, H // 4], I32, align_bytes=64)
        nc.vector.memset(w_scales_raw[:], 0)
        table_scales = keep.tile([P, T // 4], I32, align_bytes=64)
        nc.vector.memset(table_scales[:], 0)
        for q in range(4):
            load_rows(nc.scalar, w_scales_raw, w1_scales, q)
        w_words_raw = keep.tile([P, 2 * H], U8, tag="w_stage", align_bytes=64)
        nc.scalar.dma_start(w_words_raw[:].bitcast(I32), w1_words[0].bitcast(I32))
        gain = keep.tile([P, PACK], F32)
        nc.scalar.dma_start(gain[:], gs.rearrange("(p t) o -> p (t o)", t=PACK))
        n1_t = load_list(n1, "n1_t")
        n2_t = load_list(n2, "n2_t")
        cand_t = load_list(cand, "cand_t")
        n3_t = load_list(n3, "n3_t")
        n4_t = load_list(n4, "n4_t")
        pages = []
        for c in range(C // P):
            page = keep.tile([P, U], F32, name=f"page{c}")
            nc.sync.dma_start(page[:], mem[c * P : (c + 1) * P, :])
            pages.append(page)

        for q in range(4):
            nc.vector.tensor_copy(table_scales[32 * q : 32 * q + 4, :], scale_rows[32 * q : 32 * q + 4, :])
        tok_scales = keep.tile([P, S], U8, align_bytes=64)
        nc.vector.tensor_copy(tok_scales[:], table_scales[:].bitcast(U8).indirect(offs_t[:]))
        tok_words = keep.tile([P, S], U32, align_bytes=64)
        for h in range(2):
            nc.vector.tensor_copy(
                tok_words[:, h * HALF : (h + 1) * HALF], table_words[:].bitcast(U32).indirect(offs_t[:, 8 * h : 8 * h + 8])
            )
        w_words = []
        for t in range(PACK):
            dealt_words = keep.tile([P, P], U16, align_bytes=64, name=f"w_words{t}")
            nc.scalar.copy(dealt_words[:], w_words_raw[:].bitcast(U16)[:, t::PACK])
            w_words.append(dealt_words)
        first_scales = keep.tile([P, P], U8, align_bytes=64)
        later_scales = keep.tile([P, PACK - 1, P], U8, tag="w_stage", align_bytes=64)
        w_scales = [first_scales[:]] + [later_scales[:, t, :] for t in range(PACK - 1)]
        for t in range(PACK):
            nc.vector.tensor_copy(w_scales[t], w_scales_raw[:].bitcast(U8)[:, t::PACK])

        def project(t, cols, bank, y_t):
            acc = psum.tile([P, cols.stop - cols.start], F32, tag=f"bank{bank}", name=f"y_acc{bank}")
            nc.tensor.matmul_mx(
                out=acc[:],
                lhsT=w_words[t][:].bitcast(FP4X4),
                lhsT_scale=w_scales[t],
                rhs=tok_words[:, cols].bitcast(FP8X4),
                rhs_scale=tok_scales[:, cols],
                start=True,
                stop=True,
            )
            if t == 0:
                nc.scalar.copy(y_t[:, cols], acc[:])
            else:
                nc.vector.tensor_copy(y_t[:, cols], acc[:])

        y = [keep.tile([P, S], F32, name=f"y{t}") for t in range(PACK)]
        project(0, slice(0, HALF), 7, y[0])
        project(0, slice(HALF, S), 0, y[0])
        for t in range(1, PACK):
            project(t, slice(0, S), t, y[t])

        pairs = []
        for t in range(PACK):
            pair = keep.tile([P, 2, W], F32, tag=f"pair{t}", align_bytes=64, name=f"pair{t}")
            nc.scalar.activation(pair[:, 0, :], y[t][:].indirect(n1_t[:]), COPY)
            nc.scalar.activation(pair[:, 1, :], y[t][:].indirect(n2_t[:]), COPY)
            pairs.append(pair)

        larger = [keep.tile([P, W], F32, name=f"larger{t}") for t in range(PACK)]
        smaller = [keep.tile([P, W], F32, tag=f"smaller{t}", name=f"smaller{t}") for t in range(PACK)]
        for couple in ((0, 1), (2, 3)):
            for result, op in ((larger, ALU.max), (smaller, ALU.min)):
                for t in couple:
                    nc.vector.tensor_tensor(result[t][:], pairs[t][:, 0, :], pairs[t][:, 1, :], op)

        cand_words = keep.tile([P, C], U32, tag="pair0", align_bytes=64)
        for i in range(2):
            nc.vector.tensor_copy(
                cand_words[:, 256 * i : 256 * (i + 1)], table_words[:].bitcast(U32).indirect(cand_t[:, 16 * i : 16 * (i + 1)])
            )
        cand_scales = keep.tile([P, C], U8, tag="pair1", align_bytes=64)
        nc.vector.tensor_copy(cand_scales[:], table_scales[:].bitcast(U8).indirect(cand_t[:]))

        neg_gain = keep.tile([P, PACK], F32, tag="pair2", align_bytes=64)
        nc.vector.tensor_scalar(neg_gain[:], gain[:], -1.0, None, ALU.mult)
        dt = [keep.tile([P, S], F32, name=f"dt{t}") for t in range(PACK)]
        scaled = [keep.tile([P, S], F32, name=f"scaled{t}") for t in range(PACK)]
        z = {0: keep.tile([P, HALF, PACK], BF16, tag="z", align_bytes=64, name="z0")}

        def diff(t, h, other, result):
            nc.scalar.activation(other, dt[t][:].indirect(n3_t[:, 8 * h : 8 * h + 8]), COPY)
            nc.vector.scalar_tensor_tensor(
                result, other, neg_gain[:, t : t + 1], scaled[t][:, h * HALF : (h + 1) * HALF], ALU.mult, ALU.add
            )

        first = keep.tile([P, PACK, HALF], F32)
        for couple in ((0, 1), (2, 3)):
            for t in couple:
                nc.scalar.activation(dt[t][:].indirect(n1_t[:]), larger[t][:], COPY)
            for t in couple:
                nc.scalar.activation(dt[t][:].indirect(n2_t[:]), smaller[t][:], COPY)
                nc.vector.tensor_scalar(scaled[t][:], dt[t][:], gain[:, t : t + 1], None, ALU.mult)
            for t in couple:
                diff(t, 0, first[:, t, :], z[0][:, :, t])

        scores = [keep.tile([P, S], F32, name=f"scores{c}") for c in range(C // P)]

        def score(h):
            codes = keep.tile([P, HALF], U32, align_bytes=64, name=f"z_codes{h}")
            scales = keep.tile([P, HALF], U8, align_bytes=64, name=f"z_scales{h}")
            nc.vector.quantize_mx(
                out=codes[:].bitcast(FP8X4), scales=scales[:], in_=z[h][:].rearrange("p j t -> p (j t)")
            )
            for c in range(C // P):
                acc = psum.tile([P, HALF], F32, tag=f"bank{(4 + 4 * h + c) % 8}", name=f"s_acc{h}_{c}")
                nc.tensor.matmul_mx(
                    out=acc[:],
                    lhsT=cand_words[:, c * P : (c + 1) * P].bitcast(FP8X4),
                    lhsT_scale=cand_scales[:, c * P : (c + 1) * P],
                    rhs=codes[:].bitcast(FP8X4),
                    rhs_scale=scales[:],
                    start=True,
                    stop=True,
                )
                if (h, c) == (0, 0):
                    nc.scalar.activation(scores[c][:, :HALF], acc[:], COPY, scale=0.0625)
                else:
                    nc.vector.tensor_scalar(scores[c][:, h * HALF : (h + 1) * HALF], acc[:], 0.0625, None, ALU.mult)

        score(0)
        second = keep.tile([P, PACK, HALF], F32, tag="smaller3")
        planes = keep.tile([P, PACK, HALF], BF16, tag="z", align_bytes=64)
        z[1] = keep.tile([P, HALF, PACK], BF16, align_bytes=64, name="z1")
        for t in range(PACK):
            diff(t, 1, second[:, t, :], planes[:, t, :])
        nc.vector.tensor_copy(
            z[1][:].rearrange("p (c i) t -> p c t i", i=4), planes[:].rearrange("p t (c i) -> p c t i", i=4)
        )
        score(1)

        last = C // P - 1
        for h in range(2):
            for c in range(last):
                nc.scalar.activation(
                    pages[c][:].indirect(n4_t[:, 8 * h : 8 * h + 8]), scores[c][:, h * HALF : (h + 1) * HALF], COPY
                )
                if h == 1:
                    nc.sync.dma_start(out[c * P : (c + 1) * P, :], pages[c][:])
        nc.scalar.activation(pages[last][:].indirect(n4_t[:]), scores[last][:], COPY)
        for queue, cols in ((nc.scalar, slice(0, U // 2)), (nc.sync, slice(U // 2, U))):
            queue.dma_start(out[last * P : (last + 1) * P, cols], pages[last][:, cols])
